import numpy as np, ml_dtypes
CORES = [2,3,6,7,58,59,62,63,114,115,118,119]
N = 12
TK = 512
def gelu(z): return 0.5 * z * (1.0 + np.tanh(0.7978845608028654 * (z + 0.044715 * z ** 3)))
def setup_inputs(rng):
    return {"x": rng.standard_normal((N, 128, TK), dtype=np.float32).astype(ml_dtypes.bfloat16), "w1": (rng.standard_normal((N, 128, 128), dtype=np.float32) / 8).astype(ml_dtypes.bfloat16), "w2": (rng.standard_normal((N, 128, 128), dtype=np.float32) / 8).astype(ml_dtypes.bfloat16)}
def setup_inputs_big(rng):
    d = setup_inputs(rng)
    for k in ("x",): d[k] = (d[k].astype(np.float32) * 1024.0).astype(d[k].dtype)
    return d
def setup_inputs_small(rng):
    d = setup_inputs(rng)
    for k in ("x",): d[k] = (d[k].astype(np.float32) * (1 / 1024.0)).astype(d[k].dtype)
    return d
def setup_inputs_apart(rng):
    d = setup_inputs(rng)
    f = (10.0 ** rng.permutation(np.linspace(-1.5, 1.5, N))).astype(np.float32).reshape(N, 1, 1)
    for k in ("x",): d[k] = (d[k].astype(np.float32) * f).astype(d[k].dtype)
    return d
def reference(x, w1, w2):
    X, W1, W2 = x.astype(np.float64), w1.astype(np.float64), w2.astype(np.float64)
    y = np.zeros((N, 128, TK))
    for r in range(N):
        for j in range(N):
            y[r] += W2[j].T @ (gelu(W1[j].T @ X[r]))
    return {"y": y.astype(ml_dtypes.bfloat16)}

@@ -1,0 +1,207 @@
+from concourse.bass import DstId, RemoteDMATransfer
+from concourse.mybir import AluOpType, ActivationFunctionType
+
+N = 12
+TK = 512
+WW = 256
+NH = 2
+HC = TK // NH
+NPH = 6
+LOOK = 2
+
+ROLE = {}
+ORDER = [("own", 0), ("loc", 3), ("loc", 2), ("loc", 1), ("dirA", 0), ("dirB", 0),
+         ("fwdA", 3), ("fwdA", 2), ("fwdA", 1), ("fwdB", 3), ("fwdB", 2), ("fwdB", 1)]
+
+SCRATCH = {
+    "wall": ("sbuf", [128, N * WW], "bfloat16"),
+    "xs": ("sbuf", [128, TK], "bfloat16"),
+    "hb": ("sbuf", [128, N * TK], "bfloat16"),
+    "ysb": ("sbuf", [128, TK], "bfloat16"),
+    "pin": ("sbuf", [128, TK], "bfloat16"),
+    "py0": ("psum", [128, 512], "float32"),
+    "py1": ("psum", [128, 512], "float32"),
+}
+for _i in range(NPH):
+    SCRATCH["ph%d" % _i] = ("psum", [128, 512], "float32")
+
+SEMAPHORES = (["w", "x", "loc", "p", "y0", "y1", "e0", "e1", "s0", "s1"]
+              + ["r%d" % _j for _j in range(N)]
+              + ["m%d" % _i for _i in range(N * NH)]
+              + ["a%d" % _i for _i in range(N * NH)])
+
+
+def _count(mask):
+    return bin(mask).count("1")
+
+
+def _plan(T, topo):
+    cores = [int(c) for c in T.cores]
+    every = range(topo.CHIPS * topo.CORES_PER_CHIP)
+    chips = []
+    for c in cores:
+        if topo.chip(c) not in chips:
+            chips.append(topo.chip(c))
+    pairs, place = {}, {}
+    for ch in chips:
+        idle = [c for c in every if topo.chip(c) == ch and c not in cores]
+        pairs[ch] = []
+        seen = {}
+        for r in [c for c in cores if topo.chip(c) == ch]:
+            h = [c for c in idle if topo.die(c) == topo.die(r)][0]
+            idle.remove(h)
+            k = seen.get(topo.die(r), 0)
+            seen[topo.die(r)] = k + 1
+            place[r] = (topo.die(r), k)
+            pairs[ch].append((r, h))
+    npair = len(pairs[chips[0]])
+
+    def others(ch):
+        rest = [o for o in chips if o != ch]
+        return [o for o in rest if topo.same_plane(ch, o)] + [o for o in rest if not topo.same_plane(ch, o)]
+
+    def at(ch, src):
+        return [q for q, (r, _h) in enumerate(pairs[ch]) if place[r] == place[src]][0]
+
+    def kind(ch, q, j):
+        src = cores[j]
+        d = (at(ch, src) - q) % npair
+        if topo.chip(src) == ch:
+            return ("own" if d == 0 else "loc", d)
+        ab = "AB"[others(ch).index(topo.chip(src))]
+        return (("dir" if d == 0 else "fwd") + ab, d)
+
+    def cons(ch, q, j):
+        return pairs[ch][q][1 if ROLE.get(kind(ch, q, j)) == "H" else 0]
+
+    jobs, calls, arr, partner, boss = {}, {}, {}, {}, {}
+    for ch in chips:
+        for q, (r, h) in enumerate(pairs[ch]):
+            partner[r], boss[h] = h, r
+            for c in (r, h):
+                mine = [j for j in range(N) if cons(ch, q, j) == c]
+                jobs[c] = sorted(mine, key=lambda j: ORDER.index(kind(ch, q, j)))
+                calls[c] = []
+    for ch in chips:
+        for q, (r, h) in enumerate(pairs[ch]):
+            j0 = cores.index(r)
+            far = [cons(o, at(o, r), j0) for o in others(ch)][::-1]
+            near = [cons(ch, (q + o) % npair, j0) for o in range(npair)]
+            near = [c for c in near if c != r]
+            m_far = topo.mask(r, far[0])
+            for c in far:
+                m_far &= topo.mask(r, c)
+            m_near = topo.mask(r, h) & ~m_far
+            calls[r].append(("w", j0, far, m_far))
+            calls[r].append(("w", j0, near, m_near))
+            if jobs[h]:
+                calls[r].append(("x", None, [h], m_near))
+            for c in (r, h):
+                for j in jobs[c]:
+                    if kind(ch, q, j)[0] in ("dirA", "dirB"):
+                        to = [cons(ch, (q + o) % npair, j) for o in range(1, npair)]
+                        calls[c].append(("w", j, to, topo.mask(c, to[0])))
+            if jobs[h]:
+                calls[h].append(("p", None, [r], topo.mask(h, r)))
+    for c in calls:
+        for what, j, to, m in calls[c]:
+            for d in to:
+                assert topo.may_write(c, d)
+                arr[(d, what, j)] = _count(m)
+    return cores, jobs, calls, arr, partner, boss
+
+
+def rank_program(g, core, T, topo):
+    cores, jobs, calls, arr, partner, boss = _plan(T, topo)
+    if core not in jobs or not jobs[core]:
+        return
+    rank = T.rank_of(core)
+    S = T.sem
+    mine = jobs[core]
+    helped = rank is not None and bool(jobs[partner[core]])
+
+    def slot(j):
+        return T.wall[:, j * WW:(j + 1) * WW]
+
+    def here(j):
+        if rank is not None and j == rank:
+            return S.w, 32
+        return S["r%d" % j], arr[(core, "w", j)]
+
+    if rank is not None:
+        g.sync.dma_start(T.wall[:, rank * WW:rank * WW + 128], T.w1[:, :]).then_inc(S.w, 16)
+        g.scalar.dma_start(T.wall[:, rank * WW + 128:(rank + 1) * WW], T.w2[:, :]).then_inc(S.w, 16)
+        g.sync.dma_start(T.xs[:, :], T.x[:, :]).then_inc(S.x, 16)
+        x_ready = 16
+    else:
+        x_ready = arr[(core, "x", None)]
+
+    left = 0
+    for what, j, to, m in calls[core]:
+        if what == "w":
+            sem, val = here(j)
+            g.wait_ge(sem, val)
+            src, dst, rsem = slot(j), slot(j), S["r%d" % j]
+        elif what == "x":
+            g.wait_ge(S.x, x_ready)
+            src, dst, rsem = T.xs[:, :], T.xs[:, :], S.x
+        else:
+            g.wait_ge(S.e0, 1)
+            g.wait_ge(S.e1, 1)
+            src, dst, rsem = T.ysb[:, :], T.pin[:, :], S.p
+        ids = []
+        for d in to:
+            rid, pid, _ring = topo.addr(d)
+            ids.append(DstId(rid=rid, pnc=pid))
+        g.remote_dma_fused([RemoteDMATransfer(dst_ids=ids, dma_engine_mask=m, remote_sem=rsem,
+                                              srcs=[src], dsts=[dst] * len(to), alu_op=0)], local_sem=S.loc)
+        left += _count(m)
+    if left:
+        g.wait_ge(S.loc, left)
+
+    nhalf = len(mine) * NH
+    py = [T.py0, T.py1]
+    sy = [S.y0, S.y1]
+
+    def ph(i):
+        return T["ph%d" % (i % NPH)][:, 0:HC]
+
+    def hb(i):
+        return T.hb[:, i * HC:(i + 1) * HC]
+
+    g.tensor.wait_ge(S.x, x_ready)
+    for s in range(nhalf + LOOK):
+        if s < nhalf:
+            k, h = divmod(s, NH)
+            j = mine[k]
+            if h == 0:
+                sem, val = here(j)
+                g.tensor.wait_ge(sem, val)
+            g.tensor.matmul(ph(s), T.wall[:, j * WW:j * WW + 128], T.xs[:, h * HC:(h + 1) * HC],
+                            True, True).then_inc(S["m%d" % s], 1)
+        i = s - LOOK
+        if i >= 0:
+            k, h = divmod(i, NH)
+            j = mine[k]
+            g.tensor.wait_ge(S["a%d" % i], 1)
+            g.tensor.matmul(py[h][:, 0:HC], T.wall[:, j * WW + 128:(j + 1) * WW], hb(i),
+                            k == 0, k == len(mine) - 1).then_inc(sy[h], 1)
+    for i in range(nhalf):
+        g.scalar.wait_ge(S["m%d" % i], 1)
+        g.scalar.activation(hb(i), ph(i), ActivationFunctionType.Gelu_apprx_tanh).then_inc(S["a%d" % i], 1)
+
+    se = [S.e0, S.e1]
+    for h in range(NH):
+        cols = slice(h * HC, (h + 1) * HC)
+        g.vector.wait_ge(sy[h], len(mine))
+        if helped:
+            g.vector.wait_ge(S.p, arr[(core, "p", None)])
+            g.vector.tensor_tensor(T.ysb[:, cols], py[h][:, 0:HC], T.pin[:, cols], AluOpType.add).then_inc(se[h], 1)
+        else:
+            g.vector.tensor_copy(T.ysb[:, cols], py[h][:, 0:HC]).then_inc(se[h], 1)
+    if rank is not None:
+        for h, (queue, done) in enumerate(((g.sync, S.s0), (g.scalar, S.s1))):
+            cols = slice(h * HC, (h + 1) * HC)
+            queue.wait_ge(se[h], 1)
+            queue.dma_start(T.y[:, cols], T.ysb[:, cols]).then_inc(done, 16)
+            queue.wait_ge(done, 16)

@@ -4,28 +4,25 @@ from concourse.mybir import AluOpType, ActivationFunctionType
 N = 12
 TK = 512
 WW = 256
+NP = 192
+NR = TK - NP
 NH = 2
-HC = TK // NH
 NPH = 6
-LOOK = 2
-
-ROLE = {}
-ORDER = [("own", 0), ("loc", 3), ("loc", 2), ("loc", 1), ("dirA", 0), ("dirB", 0),
-         ("fwdA", 3), ("fwdA", 2), ("fwdA", 1), ("fwdB", 3), ("fwdB", 2), ("fwdB", 1)]
+LOOK_R = 2
+LOOK_H = 4
 
 SCRATCH = {
     "wall": ("sbuf", [128, N * WW], "bfloat16"),
     "xs": ("sbuf", [128, TK], "bfloat16"),
     "hb": ("sbuf", [128, N * TK], "bfloat16"),
     "ysb": ("sbuf", [128, TK], "bfloat16"),
-    "pin": ("sbuf", [128, TK], "bfloat16"),
     "py0": ("psum", [128, 512], "float32"),
     "py1": ("psum", [128, 512], "float32"),
 }
 for _i in range(NPH):
     SCRATCH["ph%d" % _i] = ("psum", [128, 512], "float32")
 
-SEMAPHORES = (["w", "x", "loc", "p", "y0", "y1", "e0", "e1", "s0", "s1"]
+SEMAPHORES = (["w", "x", "xh", "loc", "p", "y0", "y1", "e0", "e1", "s0", "s1", "s2"]
               + ["r%d" % _j for _j in range(N)]
               + ["m%d" % _i for _i in range(N * NH)]
               + ["a%d" % _i for _i in range(N * NH)])
@@ -42,10 +39,11 @@ def _plan(T, topo):
     for c in cores:
         if topo.chip(c) not in chips:
             chips.append(topo.chip(c))
-    pairs, place = {}, {}
+    nchip = len(chips)
+    pairs, place, members = {}, {}, {}
     for ch in chips:
         idle = [c for c in every if topo.chip(c) == ch and c not in cores]
-        pairs[ch] = []
+        pairs[ch], members[ch] = [], []
         seen = {}
         for r in [c for c in cores if topo.chip(c) == ch]:
             h = [c for c in idle if topo.die(c) == topo.die(r)][0]
@@ -54,56 +52,54 @@ def _plan(T, topo):
             seen[topo.die(r)] = k + 1
             place[r] = (topo.die(r), k)
             pairs[ch].append((r, h))
-    npair = len(pairs[chips[0]])
+            members[ch] += [r, h]
 
-    def others(ch):
-        rest = [o for o in chips if o != ch]
-        return [o for o in rest if topo.same_plane(ch, o)] + [o for o in rest if not topo.same_plane(ch, o)]
+    def landing(ch, src, which):
+        return [p[which] for p in pairs[ch] if place[p[0]] == place[src]][0]
 
-    def at(ch, src):
-        return [q for q, (r, _h) in enumerate(pairs[ch]) if place[r] == place[src]][0]
+    def rest(ch, c):
+        m = members[ch]
+        i = m.index(c)
+        return [m[(i + o) % len(m)] for o in range(1, len(m))]
 
-    def kind(ch, q, j):
-        src = cores[j]
-        d = (at(ch, src) - q) % npair
-        if topo.chip(src) == ch:
-            return ("own" if d == 0 else "loc", d)
-        ab = "AB"[others(ch).index(topo.chip(src))]
-        return (("dir" if d == 0 else "fwd") + ab, d)
-
-    def cons(ch, q, j):
-        return pairs[ch][q][1 if ROLE.get(kind(ch, q, j)) == "H" else 0]
-
-    jobs, calls, arr, partner, boss = {}, {}, {}, {}, {}
+    calls, partner, boss, when = {}, {}, {}, {}
     for ch in chips:
-        for q, (r, h) in enumerate(pairs[ch]):
+        for c in members[ch]:
+            calls[c] = []
+            when[c] = {}
+    for i, ch in enumerate(chips):
+        for r, h in pairs[ch]:
             partner[r], boss[h] = h, r
-            for c in (r, h):
-                mine = [j for j in range(N) if cons(ch, q, j) == c]
-                jobs[c] = sorted(mine, key=lambda j: ORDER.index(kind(ch, q, j)))
-                calls[c] = []
-    for ch in chips:
-        for q, (r, h) in enumerate(pairs[ch]):
             j0 = cores.index(r)
-            far = [cons(o, at(o, r), j0) for o in others(ch)][::-1]
-            near = [cons(ch, (q + o) % npair, j0) for o in range(npair)]
-            near = [c for c in near if c != r]
+            ring = [chips[(i + o) % nchip] for o in range(1, nchip)]
+            far = [landing(o, r, min(n, 1)) for n, o in enumerate(ring)]
             m_far = topo.mask(r, far[0])
             for c in far:
                 m_far &= topo.mask(r, c)
-            m_near = topo.mask(r, h) & ~m_far
+            m_all = topo.mask(r, h)
+            m_near = m_all & ~m_far
             calls[r].append(("w", j0, far, m_far))
-            calls[r].append(("w", j0, near, m_near))
-            if jobs[h]:
-                calls[r].append(("x", None, [h], m_near))
-            for c in (r, h):
-                for j in jobs[c]:
-                    if kind(ch, q, j)[0] in ("dirA", "dirB"):
-                        to = [cons(ch, (q + o) % npair, j) for o in range(1, npair)]
-                        calls[c].append(("w", j, to, topo.mask(c, to[0])))
-            if jobs[h]:
-                calls[h].append(("p", None, [r], topo.mask(h, r)))
+            calls[r].append(("x", None, [h], m_near))
+            calls[r].append(("w", j0, rest(ch, r), m_near))
+            when[r][j0] = (0, 0)
+            for n, c in enumerate(rest(ch, r)):
+                when[c][j0] = (1, n)
+            for n, c in enumerate(far):
+                och = topo.chip(c)
+                when[c][j0] = (2, n)
+                for n2, c2 in enumerate(rest(och, c)):
+                    when[c2][j0] = (3 + n, n2)
+    for ch in chips:
+        for c in members[ch]:
+            for j in range(N):
+                if when[c][j][0] == 2:
+                    to = rest(ch, c)
+                    calls[c].append(("w", j, to, topo.mask(c, to[0])))
+        for r, h in pairs[ch]:
+            calls[h].append(("p", None, [r], topo.mask(h, r)))
+    jobs, arr = {}, {}
     for c in calls:
+        jobs[c] = sorted(range(N), key=lambda j: when[c][j])
         for what, j, to, m in calls[c]:
             for d in to:
                 assert topo.may_write(c, d)
@@ -113,25 +109,29 @@ def _plan(T, topo):
 
 def rank_program(g, core, T, topo):
     cores, jobs, calls, arr, partner, boss = _plan(T, topo)
-    if core not in jobs or not jobs[core]:
+    if core not in jobs:
         return
     rank = T.rank_of(core)
     S = T.sem
     mine = jobs[core]
-    helped = rank is not None and bool(jobs[partner[core]])
+    is_r = rank is not None
+    c0, wid = (0, NR) if is_r else (NR, NP)
+    hc = wid // NH
+    look = LOOK_R if is_r else LOOK_H
 
     def slot(j):
         return T.wall[:, j * WW:(j + 1) * WW]
 
     def here(j):
-        if rank is not None and j == rank:
+        if is_r and j == rank:
             return S.w, 32
         return S["r%d" % j], arr[(core, "w", j)]
 
-    if rank is not None:
+    if is_r:
         g.sync.dma_start(T.wall[:, rank * WW:rank * WW + 128], T.w1[:, :]).then_inc(S.w, 16)
         g.scalar.dma_start(T.wall[:, rank * WW + 128:(rank + 1) * WW], T.w2[:, :]).then_inc(S.w, 16)
-        g.sync.dma_start(T.xs[:, :], T.x[:, :]).then_inc(S.x, 16)
+        g.sync.dma_start(T.xs[:, NR:TK], T.x[:, NR:TK]).then_inc(S.xh, 16)
+        g.scalar.dma_start(T.xs[:, 0:NR], T.x[:, 0:NR]).then_inc(S.x, 16)
         x_ready = 16
     else:
         x_ready = arr[(core, "x", None)]
@@ -143,12 +143,12 @@ def rank_program(g, core, T, topo):
             g.wait_ge(sem, val)
             src, dst, rsem = slot(j), slot(j), S["r%d" % j]
         elif what == "x":
-            g.wait_ge(S.x, x_ready)
-            src, dst, rsem = T.xs[:, :], T.xs[:, :], S.x
+            g.wait_ge(S.xh, 16)
+            src, dst, rsem = T.xs[:, NR:TK], T.xs[:, NR:TK], S.x
         else:
             g.wait_ge(S.e0, 1)
             g.wait_ge(S.e1, 1)
-            src, dst, rsem = T.ysb[:, :], T.pin[:, :], S.p
+            src, dst, rsem = T.ysb[:, NR:TK], T.ysb[:, NR:TK], S.p
         ids = []
         for d in to:
             rid, pid, _ring = topo.addr(d)
@@ -156,35 +156,34 @@ def rank_program(g, core, T, topo):
         g.remote_dma_fused([RemoteDMATransfer(dst_ids=ids, dma_engine_mask=m, remote_sem=rsem,
                                               srcs=[src], dsts=[dst] * len(to), alu_op=0)], local_sem=S.loc)
         left += _count(m)
-    if left:
-        g.wait_ge(S.loc, left)
+    g.wait_ge(S.loc, left)
 
     nhalf = len(mine) * NH
     py = [T.py0, T.py1]
     sy = [S.y0, S.y1]
 
     def ph(i):
-        return T["ph%d" % (i % NPH)][:, 0:HC]
+        return T["ph%d" % (i % NPH)][:, 0:hc]
 
     def hb(i):
-        return T.hb[:, i * HC:(i + 1) * HC]
+        return T.hb[:, i * hc:(i + 1) * hc]
 
     g.tensor.wait_ge(S.x, x_ready)
-    for s in range(nhalf + LOOK):
+    for s in range(nhalf + look):
         if s < nhalf:
             k, h = divmod(s, NH)
             j = mine[k]
             if h == 0:
                 sem, val = here(j)
                 g.tensor.wait_ge(sem, val)
-            g.tensor.matmul(ph(s), T.wall[:, j * WW:j * WW + 128], T.xs[:, h * HC:(h + 1) * HC],
+            g.tensor.matmul(ph(s), T.wall[:, j * WW:j * WW + 128], T.xs[:, c0 + h * hc:c0 + (h + 1) * hc],
                             True, True).then_inc(S["m%d" % s], 1)
-        i = s - LOOK
+        i = s - look
         if i >= 0:
             k, h = divmod(i, NH)
             j = mine[k]
             g.tensor.wait_ge(S["a%d" % i], 1)
-            g.tensor.matmul(py[h][:, 0:HC], T.wall[:, j * WW + 128:(j + 1) * WW], hb(i),
+            g.tensor.matmul(py[h][:, 0:hc], T.wall[:, j * WW + 128:(j + 1) * WW], hb(i),
                             k == 0, k == len(mine) - 1).then_inc(sy[h], 1)
     for i in range(nhalf):
         g.scalar.wait_ge(S["m%d" % i], 1)
@@ -192,16 +191,15 @@ def rank_program(g, core, T, topo):
 
     se = [S.e0, S.e1]
     for h in range(NH):
-        cols = slice(h * HC, (h + 1) * HC)
+        cols = slice(c0 + h * hc, c0 + (h + 1) * hc)
         g.vector.wait_ge(sy[h], len(mine))
-        if helped:
-            g.vector.wait_ge(S.p, arr[(core, "p", None)])
-            g.vector.tensor_tensor(T.ysb[:, cols], py[h][:, 0:HC], T.pin[:, cols], AluOpType.add).then_inc(se[h], 1)
-        else:
-            g.vector.tensor_copy(T.ysb[:, cols], py[h][:, 0:HC]).then_inc(se[h], 1)
-    if rank is not None:
+        g.vector.tensor_copy(T.ysb[:, cols], py[h][:, 0:hc]).then_inc(se[h], 1)
+    if is_r:
+        g.sync.wait_ge(S.p, arr[(core, "p", None)])
+        g.sync.dma_start(T.y[:, NR:TK], T.ysb[:, NR:TK]).then_inc(S.s2, 16)
         for h, (queue, done) in enumerate(((g.sync, S.s0), (g.scalar, S.s1))):
-            cols = slice(h * HC, (h + 1) * HC)
+            cols = slice(h * hc, (h + 1) * hc)
             queue.wait_ge(se[h], 1)
             queue.dma_start(T.y[:, cols], T.ysb[:, cols]).then_inc(done, 16)
             queue.wait_ge(done, 16)
+        g.sync.wait_ge(S.s2, 16)

from concourse.bass import DstId, RemoteDMATransfer
from concourse.mybir import AluOpType, ActivationFunctionType

N = 12
TK = 512
WW = 256
NP = 192
NR = TK - NP
NH = 2
NPH = 6
LOOK_R = 2
LOOK_H = 4

SCRATCH = {
    "wall": ("sbuf", [128, N * WW], "bfloat16"),
    "xs": ("sbuf", [128, TK], "bfloat16"),
    "hb": ("sbuf", [128, N * TK], "bfloat16"),
    "ysb": ("sbuf", [128, TK], "bfloat16"),
    "py0": ("psum", [128, 512], "float32"),
    "py1": ("psum", [128, 512], "float32"),
}
for _i in range(NPH):
    SCRATCH["ph%d" % _i] = ("psum", [128, 512], "float32")

SEMAPHORES = (["w", "x", "xh", "loc", "p", "y0", "y1", "e0", "e1", "s0", "s1", "s2"]
              + ["r%d" % _j for _j in range(N)]
              + ["m%d" % _i for _i in range(N * NH)]
              + ["a%d" % _i for _i in range(N * NH)])


def _count(mask):
    return bin(mask).count("1")


def _plan(T, topo):
    cores = [int(c) for c in T.cores]
    every = range(topo.CHIPS * topo.CORES_PER_CHIP)
    chips = []
    for c in cores:
        if topo.chip(c) not in chips:
            chips.append(topo.chip(c))
    nchip = len(chips)
    pairs, place, members = {}, {}, {}
    for ch in chips:
        idle = [c for c in every if topo.chip(c) == ch and c not in cores]
        pairs[ch], members[ch] = [], []
        seen = {}
        for r in [c for c in cores if topo.chip(c) == ch]:
            h = [c for c in idle if topo.die(c) == topo.die(r)][0]
            idle.remove(h)
            k = seen.get(topo.die(r), 0)
            seen[topo.die(r)] = k + 1
            place[r] = (topo.die(r), k)
            pairs[ch].append((r, h))
            members[ch] += [r, h]

    def landing(ch, src, which):
        return [p[which] for p in pairs[ch] if place[p[0]] == place[src]][0]

    def rest(ch, c):
        m = members[ch]
        i = m.index(c)
        return [m[(i + o) % len(m)] for o in range(1, len(m))]

    calls, partner, boss, when = {}, {}, {}, {}
    for ch in chips:
        for c in members[ch]:
            calls[c] = []
            when[c] = {}
    for i, ch in enumerate(chips):
        for r, h in pairs[ch]:
            partner[r], boss[h] = h, r
            j0 = cores.index(r)
            ring = [chips[(i + o) % nchip] for o in range(1, nchip)]
            far = [landing(o, r, min(n, 1)) for n, o in enumerate(ring)]
            m_far = topo.mask(r, far[0])
            for c in far:
                m_far &= topo.mask(r, c)
            m_all = topo.mask(r, h)
            m_near = m_all & ~m_far
            calls[r].append(("w", j0, far, m_far))
            calls[r].append(("x", None, [h], m_near))
            calls[r].append(("w", j0, rest(ch, r), m_near))
            when[r][j0] = (0, 0)
            for n, c in enumerate(rest(ch, r)):
                when[c][j0] = (1, n)
            for n, c in enumerate(far):
                och = topo.chip(c)
                when[c][j0] = (2, n)
                for n2, c2 in enumerate(rest(och, c)):
                    when[c2][j0] = (3 + n, n2)
    for ch in chips:
        for c in members[ch]:
            for j in range(N):
                if when[c][j][0] == 2:
                    to = rest(ch, c)
                    calls[c].append(("w", j, to, topo.mask(c, to[0])))
        for r, h in pairs[ch]:
            calls[h].append(("p", None, [r], topo.mask(h, r)))
    jobs, arr = {}, {}
    for c in calls:
        jobs[c] = sorted(range(N), key=lambda j: when[c][j])
        for what, j, to, m in calls[c]:
            for d in to:
                assert topo.may_write(c, d)
                arr[(d, what, j)] = _count(m)
    return cores, jobs, calls, arr, partner, boss


def rank_program(g, core, T, topo):
    cores, jobs, calls, arr, partner, boss = _plan(T, topo)
    if core not in jobs:
        return
    rank = T.rank_of(core)
    S = T.sem
    mine = jobs[core]
    is_r = rank is not None
    c0, wid = (0, NR) if is_r else (NR, NP)
    hc = wid // NH
    look = LOOK_R if is_r else LOOK_H

    def slot(j):
        return T.wall[:, j * WW:(j + 1) * WW]

    def here(j):
        if is_r and j == rank:
            return S.w, 32
        return S["r%d" % j], arr[(core, "w", j)]

    if is_r:
        g.sync.dma_start(T.wall[:, rank * WW:rank * WW + 128], T.w1[:, :]).then_inc(S.w, 16)
        g.scalar.dma_start(T.wall[:, rank * WW + 128:(rank + 1) * WW], T.w2[:, :]).then_inc(S.w, 16)
        g.sync.dma_start(T.xs[:, NR:TK], T.x[:, NR:TK]).then_inc(S.xh, 16)
        g.scalar.dma_start(T.xs[:, 0:NR], T.x[:, 0:NR]).then_inc(S.x, 16)
        x_ready = 16
    else:
        x_ready = arr[(core, "x", None)]

    left = 0
    for what, j, to, m in calls[core]:
        if what == "w":
            sem, val = here(j)
            g.wait_ge(sem, val)
            src, dst, rsem = slot(j), slot(j), S["r%d" % j]
        elif what == "x":
            g.wait_ge(S.xh, 16)
            src, dst, rsem = T.xs[:, NR:TK], T.xs[:, NR:TK], S.x
        else:
            g.wait_ge(S.e0, 1)
            g.wait_ge(S.e1, 1)
            src, dst, rsem = T.ysb[:, NR:TK], T.ysb[:, NR:TK], S.p
        ids = []
        for d in to:
            rid, pid, _ring = topo.addr(d)
            ids.append(DstId(rid=rid, pnc=pid))
        g.remote_dma_fused([RemoteDMATransfer(dst_ids=ids, dma_engine_mask=m, remote_sem=rsem,
                                              srcs=[src], dsts=[dst] * len(to), alu_op=0)], local_sem=S.loc)
        left += _count(m)
    g.wait_ge(S.loc, left)

    nhalf = len(mine) * NH
    py = [T.py0, T.py1]
    sy = [S.y0, S.y1]

    def ph(i):
        return T["ph%d" % (i % NPH)][:, 0:hc]

    def hb(i):
        return T.hb[:, i * hc:(i + 1) * hc]

    g.tensor.wait_ge(S.x, x_ready)
    for s in range(nhalf + look):
        if s < nhalf:
            k, h = divmod(s, NH)
            j = mine[k]
            if h == 0:
                sem, val = here(j)
                g.tensor.wait_ge(sem, val)
            g.tensor.matmul(ph(s), T.wall[:, j * WW:j * WW + 128], T.xs[:, c0 + h * hc:c0 + (h + 1) * hc],
                            True, True).then_inc(S["m%d" % s], 1)
        i = s - look
        if i >= 0:
            k, h = divmod(i, NH)
            j = mine[k]
            g.tensor.wait_ge(S["a%d" % i], 1)
            g.tensor.matmul(py[h][:, 0:hc], T.wall[:, j * WW + 128:(j + 1) * WW], hb(i),
                            k == 0, k == len(mine) - 1).then_inc(sy[h], 1)
    for i in range(nhalf):
        g.scalar.wait_ge(S["m%d" % i], 1)
        g.scalar.activation(hb(i), ph(i), ActivationFunctionType.Gelu_apprx_tanh).then_inc(S["a%d" % i], 1)

    se = [S.e0, S.e1]
    for h in range(NH):
        cols = slice(c0 + h * hc, c0 + (h + 1) * hc)
        g.vector.wait_ge(sy[h], len(mine))
        g.vector.tensor_copy(T.ysb[:, cols], py[h][:, 0:hc]).then_inc(se[h], 1)
    if is_r:
        g.sync.wait_ge(S.p, arr[(core, "p", None)])
        g.sync.dma_start(T.y[:, NR:TK], T.ysb[:, NR:TK]).then_inc(S.s2, 16)
        for h, (queue, done) in enumerate(((g.sync, S.s0), (g.scalar, S.s1))):
            cols = slice(h * hc, (h + 1) * hc)
            queue.wait_ge(se[h], 1)
            queue.dma_start(T.y[:, cols], T.ysb[:, cols]).then_inc(done, 16)
            queue.wait_ge(done, 16)
        g.sync.wait_ge(S.s2, 16)
